import numpy as np
import ml_dtypes


def mxq(x, axis, fmt="e4m3"):
    dtype, down = {"e4m3": (ml_dtypes.float8_e4m3fn, 7), "e5m2": (ml_dtypes.float8_e5m2, 14)}[fmt]
    v = np.moveaxis(np.asarray(x, np.float32).astype(ml_dtypes.bfloat16).astype(np.float64), axis, -1)
    blocks = v.reshape(v.shape[:-1] + (-1, 32))
    amax = np.abs(blocks).max(-1, keepdims=True)
    byte = np.maximum(np.where(amax > 0, np.frexp(amax)[1] - 1 + 127, 0) - down, 1)
    scale = np.exp2(byte - 127.0)
    codes = (blocks / scale).astype(np.float32).astype(dtype).astype(np.float64)
    return np.moveaxis((codes * scale).reshape(v.shape), -1, axis)


WIDE = False


def mx_kscale(k):
    if not WIDE:
        return np.ones(k)
    levels = np.array([10, -10, 5, -5, 0])
    if k % 512:
        return np.exp2(np.random.permutation(np.resize(levels, k // 32))).repeat(32)
    a = np.empty((k // 512, 16))
    for p in range(k // 512):
        a[p, :8] = np.random.permutation(np.resize(levels, 8))
        for g in range(8):
            far = levels[np.abs(levels - a[p, g]) >= 10]
            a[p, g + 8] = far[np.random.randint(len(far))]
    return np.exp2(a.ravel()).repeat(32)


def f64(x):
    return np.asarray(x).astype(np.float64)


def striped(idx):
    return np.tile(idx.reshape(-1, 16).T, (8, 1)).astype(np.uint16)


def unstriped(offs):
    return offs[:16].T.reshape(-1).astype(np.int64)


def striped8(idx):
    return np.concatenate([x.reshape(-1, 16).T for x in idx]).astype(np.uint16)


def runs(offs, k):
    lists = np.stack([offs[16 * r : 16 * r + 16].T.reshape(-1) for r in range(8)]).astype(np.int64)
    return lists[np.arange(k) % 512 // 64]


def pack_weight(w):
    k, n = w.shape
    w = f64(np.asarray(w, np.float32).astype(ml_dtypes.bfloat16)).reshape(k // 32, 32, n)
    amax = np.abs(w).max(1)
    byte = np.clip(np.where(amax > 0, np.frexp(amax)[1] - 1 + 127 - 7, 1), 1, 254)
    scaled = (w * np.exp2(127.0 - byte)[:, None, :]).reshape(k, n).astype(np.float32)
    words = np.ascontiguousarray(scaled.reshape(k // 512, 128, 4, n).transpose(0, 1, 3, 2)).astype(ml_dtypes.float8_e4m3fn).view(np.uint8)
    return words, np.ascontiguousarray(byte.astype(np.uint8).reshape(k // 512, 16, n))


def unpack_weight(words, scales):
    g, p, n, _ = words.shape
    vals = np.ascontiguousarray(words).view(ml_dtypes.float8_e4m3fn).astype(np.float64) * np.repeat(np.exp2(scales.astype(np.float64) - 127.0), 8, axis=1)[..., None]
    return vals.transpose(0, 1, 3, 2).reshape(g * 512, n)


K, T, S, G, H, C = 512, 1024, 256, 2048, 512, 512


def setup_inputs():
    n = np.random.standard_normal
    s = mx_kscale(K)[:, None]
    packed_xT = pack_weight(n((K, T)) * s)
    packed_dT = pack_weight(n((K, G)) / s)
    return {
        "x_words": packed_xT[0],
        "x_scales": packed_xT[1],
        "d_words": packed_dT[0],
        "d_scales": packed_dT[1],
        "gs": (np.random.uniform(0.5, 1.5, (K, 1)) / s).astype(np.float32),
        "offs": striped(np.random.permutation(T)[:S]),
        "ka": striped8(np.random.randint(0, G, (8, H))),
        "kb": striped8(np.random.randint(0, G, (8, H))),
        "cand": striped(np.random.permutation(T)[:C]),
        "n1": striped(np.random.permutation(S)),
        "n2": striped(np.random.permutation(S)),
    }


def reference(x_words, x_scales, d_words, d_scales, gs, offs, ka, kb, cand, n1, n2):
    x_cand = unpack_weight(x_words, x_scales)[:, unstriped(cand)]
    d_ka = unpack_weight(d_words, d_scales)[np.arange(K)[:, None], runs(ka, K)]
    xq = unpack_weight(x_words, x_scales)[:, unstriped(offs)]
    d_kb = unpack_weight(d_words, d_scales)[np.arange(K)[:, None], runs(kb, K)]
    h = 0.0625 * (d_ka.T @ xq + d_kb.T @ xq)
    z = f64(gs) * h
    s = 0.0625 * ((x_cand.T @ mxq(z, 0, "e4m3")))
    ds = np.zeros((C, S))
    ds[:, unstriped(n1)] = s
    ds2 = np.zeros((C, S))
    ds2[:, unstriped(n2)] = s
    return np.maximum(ds, ds2)

@@ -1,0 +1,194 @@
+from contextlib import ExitStack
+
+import concourse.mybir as mybir
+from concourse.masks import make_identity
+
+K, T, S, G, H, C = 512, 1024, 256, 2048, 512, 512
+FLOPS = 2 * K * H * S * 2 + 2 * H * C * S
+
+F32 = mybir.dt.float32
+BF16 = mybir.dt.bfloat16
+I32 = mybir.dt.int32
+U32 = mybir.dt.uint32
+U16 = mybir.dt.uint16
+U8 = mybir.dt.uint8
+FP8X4 = mybir.dt.float8_e4m3fn_x4
+COPY = mybir.ActivationFunctionType.Copy
+MULT = mybir.AluOpType.mult
+MAX = mybir.AluOpType.max
+
+P = 128
+SIXTEENTH = 0.0625
+
+
+def tile_picked_aqcisendtwo_none_p_kernel(tc, x_words, x_scales, d_words, d_scales, gs, offs, ka, kb, cand, n1, n2, out):
+    nc = tc.nc
+
+    def cols(lst, start, count):
+        return lst[:, start // 16 : (start + count) // 16]
+
+    with ExitStack() as ctx:
+        lists = ctx.enter_context(tc.tile_pool(name="lists", bufs=1))
+        keep = ctx.enter_context(tc.tile_pool(name="keep", bufs=1))
+        share = ctx.enter_context(tc.tile_pool(name="share", bufs=1))
+        psum = ctx.enter_context(tc.psum_pool(name="psum", bufs=1))
+
+        ka_l = lists.tile([P, H // 16], U16, name="ka_l")
+        kb_l = lists.tile([P, H // 16], U16, name="kb_l")
+        offs_l = lists.tile([P, S // 16], U16, name="offs_l")
+        cand_l = lists.tile([P, C // 16], U16, name="cand_l")
+        n1_l = lists.tile([P, S // 16], U16, name="n1_l")
+        n2_l = lists.tile([P, S // 16], U16, name="n2_l")
+
+        d_word_tab = keep.tile([P, G], U32, name="d_word_tab", align_bytes=64)
+        d_byte_tab = keep.tile([P, G], U8, name="d_byte_tab", align_bytes=64)
+        x_word_tab = keep.tile([P, T], U32, name="x_word_tab", align_bytes=64)
+        x_byte_tab = keep.tile([P, T], U8, name="x_byte_tab", align_bytes=64)
+        gs_col = keep.tile([P, 4], F32, name="gs_col")
+
+        nc.sync.dma_start(
+            d_byte_tab[:].bitcast(I32),
+            d_scales[0].bitcast(I32).unsqueeze(1).to_broadcast([16, 8, G // 4]),
+        )
+        nc.sync.dma_start(ka_l[:], ka)
+        nc.sync.dma_start(kb_l[:], kb)
+        nc.sync.dma_start(d_word_tab[:].bitcast(I32), d_words[0].rearrange("p n t -> p (n t)").bitcast(I32))
+        for q in range(4):
+            nc.scalar.dma_start(
+                x_byte_tab[32 * q : 32 * q + 32, :].bitcast(I32),
+                x_scales[0, 4 * q : 4 * q + 4, :].bitcast(I32).unsqueeze(0).to_broadcast([8, 4, T // 4]),
+            )
+        nc.scalar.dma_start(gs_col[:], gs.rearrange("(p t) o -> p (t o)", t=4))
+        nc.sync.dma_start(offs_l[:], offs)
+        nc.sync.dma_start(x_word_tab[:].bitcast(I32), x_words[0].rearrange("p n t -> p (n t)").bitcast(I32))
+        nc.sync.dma_start(cand_l[:], cand)
+        nc.sync.dma_start(n1_l[:], n1)
+        nc.sync.dma_start(n2_l[:], n2)
+
+        d_plane = keep.tile([P, 2 * H], U8, name="d_plane", align_bytes=64)
+        nc.vector.memset(d_plane[:].bitcast(I32), 0)
+        ident = keep.tile([P, P], F32, name="ident")
+        nc.vector.memset(ident[:], 0.0)
+        make_identity(nc, ident[:], nomemset=True)
+
+        gs_ps = psum.tile([P, 4, P], F32, name="gs_ps", tag="turn", bufs=2)
+        for t in range(4):
+            nc.tensor.transpose(gs_ps[:, t, :], gs_col[:, t : t + 1].to_broadcast([P, P]), ident[:])
+        gs_row = keep.tile([P, 2, P, 2], F32, name="gs_row")
+        nc.scalar.activation(gs_row[:], gs_ps[:].rearrange("p (u e) m -> p u m e", e=2), COPY, scale=SIXTEENTH)
+
+        d_bytes = keep.tile([P, 2 * H], U8, name="d_bytes", align_bytes=64)
+        nc.vector.tensor_copy(d_bytes[:, 0:H], d_byte_tab[:].indirect(ka_l[:]))
+        nc.vector.tensor_copy(d_bytes[:, H : 2 * H], d_byte_tab[:].indirect(kb_l[:]))
+        for i in range(4):
+            nc.sync.dma_start(d_plane[i:P:32, :].bitcast(I32), d_bytes[8 * i : P : 32, :].bitcast(I32))
+
+        d_a = keep.tile([P, H], U32, name="d_a", align_bytes=64)
+        d_b = keep.tile([P, H], U32, name="d_b", align_bytes=64)
+        nc.vector.tensor_copy(d_a[:], d_word_tab[:].indirect(ka_l[:]))
+
+        place = {
+            "xq0_w": 0, "xq0_b": 512, "xc0_w": 0, "xc0_b": 512,
+            "zt0": 640, "xc1_w": 640, "xc1_b": 1152,
+            "grouped0": 1664, "xq1_w": 1664, "xq1_b": 2176, "xc2_b": 2304, "xc2_w": 2560,
+        }
+
+        def tile(shape, dtype, name):
+            if name in place:
+                return share.tile(shape, dtype, name=name, align_bytes=64, offset=place[name])
+            return keep.tile(shape, dtype, name=name, align_bytes=64)
+
+        def pick_x(lst, start, name, n=P):
+            b = tile([P, n], U8, name + "_b")
+            w = tile([P, n], U32, name + "_w")
+            nc.vector.tensor_copy(b[:], x_byte_tab[:].indirect(cols(lst, start, n)))
+            nc.vector.tensor_copy(w[:], x_word_tab[:].indirect(cols(lst, start, n)))
+            return w, b
+
+        def first_product(xq, f0, n, name):
+            w, b = xq
+            bank = psum.tile([P, n], F32, name=name)
+            for j, words in enumerate((d_a, d_b)):
+                nc.tensor.matmul_mx(
+                    out=bank[:],
+                    lhsT=w[:].bitcast(FP8X4),
+                    lhsT_scale=b[:],
+                    rhs=words[:, f0 : f0 + n].bitcast(FP8X4),
+                    rhs_scale=d_plane[:, j * H + f0 : j * H + f0 + n],
+                    start=(j == 0),
+                    stop=(j == 1),
+                )
+            return bank
+
+        def weigh(zt, bank, f0, n):
+            m = slice(f0 // 4, (f0 + n) // 4)
+            nc.vector.tensor_tensor(
+                zt[:, :, m, :], bank[:].rearrange("p (m u e) -> p u m e", u=2, e=2), gs_row[:, :, m, :], MULT
+            )
+
+        def turn_and_quantize(zt, half):
+            words = zt[:].rearrange("p u m e -> p (u m e)").bitcast(F32)
+            turned = psum.tile([P, 2, P], F32, name="turned%d" % half, tag="turn", bufs=2)
+            for u in range(2):
+                nc.tensor.transpose(turned[:, u, :], words[:, u * P : (u + 1) * P], ident[:])
+            grouped = tile([P, 4 * P], BF16, "grouped%d" % half)
+            dst = grouped[:].bitcast(F32).rearrange("p (r u) -> p r u", u=2)
+            src = turned[:].rearrange("p u r -> p r u")
+            if half == 0:
+                nc.scalar.copy(dst, src)
+            else:
+                nc.vector.tensor_copy(dst, src)
+            zw = keep.tile([P, P], U32, name="zw%d" % half, align_bytes=64)
+            zb = keep.tile([P, P], U8, name="zb%d" % half, align_bytes=64)
+            nc.vector.quantize_mx(out=zw[:].bitcast(FP8X4), scales=zb[:], in_=grouped[:])
+            return zw, zb
+
+        sent = [
+            [keep.tile([P, S], F32, name="sent%d_%d" % (c, j)) for j in range(2)] for c in range(C // P)
+        ]
+
+        def score_and_send(c, half, xc, z):
+            bank = psum.tile([P, P], F32, name="s_ps", tag="s_ps", bufs=3)
+            nc.tensor.matmul_mx(
+                out=bank[:],
+                lhsT=xc[0].bitcast(FP8X4),
+                lhsT_scale=xc[1],
+                rhs=z[0][:].bitcast(FP8X4),
+                rhs_scale=z[1][:],
+                start=True,
+                stop=True,
+            )
+            s_sb = tile([P, P], F32, "s%d_%d" % (c, half))
+            nc.vector.tensor_scalar(s_sb[:], bank[:], SIXTEENTH, None, MULT)
+            for j, lst in enumerate((n1_l, n2_l)):
+                nc.scalar.activation(sent[c][j][:].indirect(cols(lst, half * P, P)), s_sb[:], COPY)
+
+        xq0 = pick_x(offs_l, 0, "xq0")
+        zt0 = tile([P, 2, P, 2], BF16, "zt0")
+        banks = []
+        for f0 in (0, H // 2):
+            nc.vector.tensor_copy(d_b[:, f0 : f0 + H // 2], d_word_tab[:].indirect(cols(kb_l, f0, H // 2)))
+            banks.append(first_product(xq0, f0, H // 2, "h0_%d" % f0))
+        for bank, f0 in zip(banks, (0, H // 2)):
+            weigh(zt0, bank, f0, H // 2)
+        w, b = pick_x(cand_l, 0, "xc0")
+        xc = [(w[:], b[:])]
+        z0 = turn_and_quantize(zt0, 0)
+        score_and_send(0, 0, xc[0], z0)
+        w, b = pick_x(cand_l, P, "xc1")
+        xc.append((w[:], b[:]))
+        score_and_send(1, 0, xc[1], z0)
+        xq1 = pick_x(offs_l, P, "xq1")
+        w, b = pick_x(cand_l, 2 * P, "xc2", 2 * P)
+        for c in range(2):
+            xc.append((w[:, c * P : (c + 1) * P], b[:, c * P : (c + 1) * P]))
+            score_and_send(2 + c, 0, xc[2 + c], z0)
+        bank1 = first_product(xq1, 0, H, "h1")
+        zt1 = keep.tile([P, 2, P, 2], BF16, name="zt1")
+        weigh(zt1, bank1, 0, H)
+        z1 = turn_and_quantize(zt1, 1)
+        for c in range(C // P):
+            score_and_send(c, 1, xc[c], z1)
+            res = keep.tile([P, S], F32, name="res%d" % c)
+            nc.vector.tensor_tensor(res[:], sent[c][0][:], sent[c][1][:], MAX)
+            nc.sync.dma_start(out[c * P : (c + 1) * P, :], res[:])

@@ -44,53 +44,32 @@ def tile_picked_aqcisendtwo_none_p_kernel(tc, x_words, x_scales, d_words, d_scal
         d_byte_tab = keep.tile([P, G], U8, name="d_byte_tab", align_bytes=64)
         x_word_tab = keep.tile([P, T], U32, name="x_word_tab", align_bytes=64)
         x_byte_tab = keep.tile([P, T], U8, name="x_byte_tab", align_bytes=64)
+        x_byte_rows = keep.tile([P, T], U8, name="x_byte_rows", align_bytes=64)
         gs_col = keep.tile([P, 4], F32, name="gs_col")
 
-        nc.sync.dma_start(
-            d_byte_tab[:].bitcast(I32),
-            d_scales[0].bitcast(I32).unsqueeze(1).to_broadcast([16, 8, G // 4]),
-        )
+        def load_bytes(tab, scales):
+            rows = scales[0].bitcast(I32)
+            nc.scalar.dma_start(tab[:].bitcast(I32), rows.unsqueeze(1).to_broadcast([16, 8, rows.shape[1]]))
+
+        def load_words(tab, words):
+            nc.sync.dma_start(tab[:].bitcast(I32), words[0].rearrange("p n t -> p (n t)").bitcast(I32))
+
         nc.sync.dma_start(ka_l[:], ka)
+        load_bytes(d_byte_tab, d_scales)
         nc.sync.dma_start(kb_l[:], kb)
-        nc.sync.dma_start(d_word_tab[:].bitcast(I32), d_words[0].rearrange("p n t -> p (n t)").bitcast(I32))
-        for q in range(4):
-            nc.scalar.dma_start(
-                x_byte_tab[32 * q : 32 * q + 32, :].bitcast(I32),
-                x_scales[0, 4 * q : 4 * q + 4, :].bitcast(I32).unsqueeze(0).to_broadcast([8, 4, T // 4]),
-            )
-        nc.scalar.dma_start(gs_col[:], gs.rearrange("(p t) o -> p (t o)", t=4))
+        load_bytes(x_byte_tab, x_scales)
         nc.sync.dma_start(offs_l[:], offs)
-        nc.sync.dma_start(x_word_tab[:].bitcast(I32), x_words[0].rearrange("p n t -> p (n t)").bitcast(I32))
+        nc.sync.dma_start(gs_col[:], gs.rearrange("(p t) o -> p (t o)", t=4))
+        load_words(x_word_tab, x_words)
+        load_words(d_word_tab, d_words)
         nc.sync.dma_start(cand_l[:], cand)
         nc.sync.dma_start(n1_l[:], n1)
         nc.sync.dma_start(n2_l[:], n2)
 
-        d_plane = keep.tile([P, 2 * H], U8, name="d_plane", align_bytes=64)
-        nc.vector.memset(d_plane[:].bitcast(I32), 0)
-        ident = keep.tile([P, P], F32, name="ident")
-        nc.vector.memset(ident[:], 0.0)
-        make_identity(nc, ident[:], nomemset=True)
-
-        gs_ps = psum.tile([P, 4, P], F32, name="gs_ps", tag="turn", bufs=2)
-        for t in range(4):
-            nc.tensor.transpose(gs_ps[:, t, :], gs_col[:, t : t + 1].to_broadcast([P, P]), ident[:])
-        gs_row = keep.tile([P, 2, P, 2], F32, name="gs_row")
-        nc.scalar.activation(gs_row[:], gs_ps[:].rearrange("p (u e) m -> p u m e", e=2), COPY, scale=SIXTEENTH)
-
-        d_bytes = keep.tile([P, 2 * H], U8, name="d_bytes", align_bytes=64)
-        nc.vector.tensor_copy(d_bytes[:, 0:H], d_byte_tab[:].indirect(ka_l[:]))
-        nc.vector.tensor_copy(d_bytes[:, H : 2 * H], d_byte_tab[:].indirect(kb_l[:]))
-        for i in range(4):
-            nc.sync.dma_start(d_plane[i:P:32, :].bitcast(I32), d_bytes[8 * i : P : 32, :].bitcast(I32))
-
-        d_a = keep.tile([P, H], U32, name="d_a", align_bytes=64)
-        d_b = keep.tile([P, H], U32, name="d_b", align_bytes=64)
-        nc.vector.tensor_copy(d_a[:], d_word_tab[:].indirect(ka_l[:]))
-
         place = {
-            "xq0_w": 0, "xq0_b": 512, "xc0_w": 0, "xc0_b": 512,
-            "zt0": 640, "xc1_w": 640, "xc1_b": 1152,
-            "grouped0": 1664, "xq1_w": 1664, "xq1_b": 2176, "xc2_b": 2304, "xc2_w": 2560,
+            "xq0_w": 1536, "xc0_w": 1280, "xc0_b": 1792,
+            "zt0": 2048, "xq1_b": 2048,
+            "grouped0": 4096, "xc2_w": 3136, "xc1_w": 4160, "xc1_b": 4672, "xc2_b": 4800, "xq1_w": 5056,
         }
 
         def tile(shape, dtype, name):
@@ -98,32 +77,66 @@ def tile_picked_aqcisendtwo_none_p_kernel(tc, x_words, x_scales, d_words, d_scal
                 return share.tile(shape, dtype, name=name, align_bytes=64, offset=place[name])
             return keep.tile(shape, dtype, name=name, align_bytes=64)
 
-        def pick_x(lst, start, name, n=P):
-            b = tile([P, n], U8, name + "_b")
-            w = tile([P, n], U32, name + "_w")
-            nc.vector.tensor_copy(b[:], x_byte_tab[:].indirect(cols(lst, start, n)))
-            nc.vector.tensor_copy(w[:], x_word_tab[:].indirect(cols(lst, start, n)))
-            return w, b
+        early_plane = tile([P, 2 * H + P], U8, "early_plane")
+        nc.vector.memset(early_plane[:].bitcast(I32), 0)
+        ident = keep.tile([P, P], F32, name="ident")
+        make_identity(nc, ident[:])
+        nc.gpsimd.memset(x_byte_rows[:].bitcast(I32), 0)
+        for q in range(4):
+            nc.gpsimd.dma_start(
+                x_byte_rows[32 * q : 32 * q + 4, :].bitcast(I32), x_scales[0, 4 * q : 4 * q + 4, :].bitcast(I32)
+            )
 
-        def first_product(xq, f0, n, name):
-            w, b = xq
-            bank = psum.tile([P, n], F32, name=name)
-            for j, words in enumerate((d_a, d_b)):
-                nc.tensor.matmul_mx(
-                    out=bank[:],
-                    lhsT=w[:].bitcast(FP8X4),
-                    lhsT_scale=b[:],
-                    rhs=words[:, f0 : f0 + n].bitcast(FP8X4),
-                    rhs_scale=d_plane[:, j * H + f0 : j * H + f0 + n],
-                    start=(j == 0),
-                    stop=(j == 1),
-                )
-            return bank
+        gs_ps = psum.tile([P, 4, P], F32, name="gs_ps", tag="turn", bufs=2)
+        for t in range(4):
+            nc.tensor.transpose(gs_ps[:, t, :], gs_col[:, t : t + 1].to_broadcast([P, P]), ident[:])
+        gs_row = keep.tile([P, 2, P, 2], F32, name="gs_row")
+        nc.scalar.activation(gs_row[:], gs_ps[:].rearrange("p (u e) m -> p u m e", e=2), COPY, scale=SIXTEENTH)
+
+        def gather(dst, tab, lst, start, n):
+            nc.vector.tensor_copy(dst, tab[:].indirect(cols(lst, start, n)))
+
+        def to_plane(plane, picked):
+            for i in range(4):
+                nc.sync.dma_start(plane[i:P:32, :].bitcast(I32), picked[8 * i : P : 32, :].bitcast(I32))
+
+        early_bytes = tile([P, 2 * H + P], U8, "early_bytes")
+        gather(early_bytes[:, 0:H], d_byte_tab, ka_l, 0, H)
+        gather(early_bytes[:, H : 2 * H], d_byte_tab, kb_l, 0, H)
+        gather(early_bytes[:, 2 * H : 2 * H + P], x_byte_tab, offs_l, 0, P)
+        to_plane(early_plane, early_bytes)
+
+        def pick_words(tab, lst, start, n, name):
+            w = tile([P, n], U32, name)
+            gather(w[:], tab, lst, start, n)
+            return w
+
+        def pick_x(lst, start, n, name):
+            b = tile([P, n], U8, name + "_b")
+            gather(b[:], x_byte_rows, lst, start, n)
+            return pick_words(x_word_tab, lst, start, n, name + "_w"), b
+
+        xq0_w = pick_words(x_word_tab, offs_l, 0, P, "xq0_w")
+        d_a = pick_words(d_word_tab, ka_l, 0, H, "d_a")
+        d_b = [pick_words(d_word_tab, kb_l, f * (H // 2), H // 2, "d_b%d" % f) for f in range(2)]
+
+        def first_product(w, b, f, j, bank):
+            n = H // 2
+            words = (d_a[:, f * n : (f + 1) * n], d_b[f][:])[j]
+            nc.tensor.matmul_mx(
+                out=bank,
+                lhsT=w.bitcast(FP8X4),
+                lhsT_scale=b,
+                rhs=words.bitcast(FP8X4),
+                rhs_scale=early_plane[:, j * H + f * n : j * H + (f + 1) * n],
+                start=(j == 0),
+                stop=(j == 1),
+            )
 
         def weigh(zt, bank, f0, n):
             m = slice(f0 // 4, (f0 + n) // 4)
             nc.vector.tensor_tensor(
-                zt[:, :, m, :], bank[:].rearrange("p (m u e) -> p u m e", u=2, e=2), gs_row[:, :, m, :], MULT
+                zt[:, :, m, :], bank.rearrange("p (m u e) -> p u m e", u=2, e=2), gs_row[:, :, m, :], MULT
             )
 
         def turn_and_quantize(zt, half):
@@ -138,8 +151,8 @@ def tile_picked_aqcisendtwo_none_p_kernel(tc, x_words, x_scales, d_words, d_scal
                 nc.scalar.copy(dst, src)
             else:
                 nc.vector.tensor_copy(dst, src)
-            zw = keep.tile([P, P], U32, name="zw%d" % half, align_bytes=64)
-            zb = keep.tile([P, P], U8, name="zb%d" % half, align_bytes=64)
+            zw = tile([P, P], U32, "zw%d" % half)
+            zb = tile([P, P], U8, "zb%d" % half)
             nc.vector.quantize_mx(out=zw[:].bitcast(FP8X4), scales=zb[:], in_=grouped[:])
             return zw, zb
 
@@ -159,33 +172,38 @@ def tile_picked_aqcisendtwo_none_p_kernel(tc, x_words, x_scales, d_words, d_scal
                 stop=True,
             )
             s_sb = tile([P, P], F32, "s%d_%d" % (c, half))
-            nc.vector.tensor_scalar(s_sb[:], bank[:], SIXTEENTH, None, MULT)
+            if c == 0 and half == 0:
+                nc.scalar.activation(s_sb[:], bank[:], COPY, scale=SIXTEENTH)
+            else:
+                nc.vector.tensor_scalar(s_sb[:], bank[:], SIXTEENTH, None, MULT)
             for j, lst in enumerate((n1_l, n2_l)):
                 nc.scalar.activation(sent[c][j][:].indirect(cols(lst, half * P, P)), s_sb[:], COPY)
 
-        xq0 = pick_x(offs_l, 0, "xq0")
         zt0 = tile([P, 2, P, 2], BF16, "zt0")
-        banks = []
-        for f0 in (0, H // 2):
-            nc.vector.tensor_copy(d_b[:, f0 : f0 + H // 2], d_word_tab[:].indirect(cols(kb_l, f0, H // 2)))
-            banks.append(first_product(xq0, f0, H // 2, "h0_%d" % f0))
-        for bank, f0 in zip(banks, (0, H // 2)):
-            weigh(zt0, bank, f0, H // 2)
-        w, b = pick_x(cand_l, 0, "xc0")
+        banks = [psum.tile([P, H // 2], F32, name="h0_%d" % f) for f in range(2)]
+        for j in range(2):
+            for f in range(2):
+                first_product(xq0_w[:], early_plane[:, 2 * H : 2 * H + P], f, j, banks[f][:])
+        for f in range(2):
+            weigh(zt0, banks[f][:], f * (H // 2), H // 2)
+        w, b = pick_x(cand_l, 0, P, "xc0")
         xc = [(w[:], b[:])]
         z0 = turn_and_quantize(zt0, 0)
         score_and_send(0, 0, xc[0], z0)
-        w, b = pick_x(cand_l, P, "xc1")
+        w, b = pick_x(cand_l, P, P, "xc1")
         xc.append((w[:], b[:]))
         score_and_send(1, 0, xc[1], z0)
-        xq1 = pick_x(offs_l, P, "xq1")
-        w, b = pick_x(cand_l, 2 * P, "xc2", 2 * P)
+        xq1_w, xq1_b = pick_x(offs_l, P, P, "xq1")
+        w, b = pick_x(cand_l, 2 * P, 2 * P, "xc2")
         for c in range(2):
             xc.append((w[:, c * P : (c + 1) * P], b[:, c * P : (c + 1) * P]))
             score_and_send(2 + c, 0, xc[2 + c], z0)
-        bank1 = first_product(xq1, 0, H, "h1")
-        zt1 = keep.tile([P, 2, P, 2], BF16, name="zt1")
-        weigh(zt1, bank1, 0, H)
+        bank1 = psum.tile([P, H], F32, name="h1")
+        for f in range(2):
+            for j in range(2):
+                first_product(xq1_w[:], xq1_b[:], f, j, bank1[:, f * (H // 2) : (f + 1) * (H // 2)])
+        zt1 = tile([P, 2, P, 2], BF16, "zt1")
+        weigh(zt1, bank1[:], 0, H)
         z1 = turn_and_quantize(zt1, 1)
         for c in range(C // P):
             score_and_send(c, 1, xc[c], z1)

from contextlib import ExitStack

import concourse.mybir as mybir
from concourse.masks import make_identity

K, T, S, G, H, C = 512, 1024, 256, 2048, 512, 512
FLOPS = 2 * K * H * S * 2 + 2 * H * C * S

F32 = mybir.dt.float32
BF16 = mybir.dt.bfloat16
I32 = mybir.dt.int32
U32 = mybir.dt.uint32
U16 = mybir.dt.uint16
U8 = mybir.dt.uint8
FP8X4 = mybir.dt.float8_e4m3fn_x4
COPY = mybir.ActivationFunctionType.Copy
MULT = mybir.AluOpType.mult
MAX = mybir.AluOpType.max

P = 128
SIXTEENTH = 0.0625


def tile_picked_aqcisendtwo_none_p_kernel(tc, x_words, x_scales, d_words, d_scales, gs, offs, ka, kb, cand, n1, n2, out):
    nc = tc.nc

    def cols(lst, start, count):
        return lst[:, start // 16 : (start + count) // 16]

    with ExitStack() as ctx:
        lists = ctx.enter_context(tc.tile_pool(name="lists", bufs=1))
        keep = ctx.enter_context(tc.tile_pool(name="keep", bufs=1))
        share = ctx.enter_context(tc.tile_pool(name="share", bufs=1))
        psum = ctx.enter_context(tc.psum_pool(name="psum", bufs=1))

        ka_l = lists.tile([P, H // 16], U16, name="ka_l")
        kb_l = lists.tile([P, H // 16], U16, name="kb_l")
        offs_l = lists.tile([P, S // 16], U16, name="offs_l")
        cand_l = lists.tile([P, C // 16], U16, name="cand_l")
        n1_l = lists.tile([P, S // 16], U16, name="n1_l")
        n2_l = lists.tile([P, S // 16], U16, name="n2_l")

        d_word_tab = keep.tile([P, G], U32, name="d_word_tab", align_bytes=64)
        d_byte_tab = keep.tile([P, G], U8, name="d_byte_tab", align_bytes=64)
        x_word_tab = keep.tile([P, T], U32, name="x_word_tab", align_bytes=64)
        x_byte_tab = keep.tile([P, T], U8, name="x_byte_tab", align_bytes=64)
        x_byte_rows = keep.tile([P, T], U8, name="x_byte_rows", align_bytes=64)
        gs_col = keep.tile([P, 4], F32, name="gs_col")

        def load_bytes(tab, scales):
            rows = scales[0].bitcast(I32)
            nc.scalar.dma_start(tab[:].bitcast(I32), rows.unsqueeze(1).to_broadcast([16, 8, rows.shape[1]]))

        def load_words(tab, words):
            nc.sync.dma_start(tab[:].bitcast(I32), words[0].rearrange("p n t -> p (n t)").bitcast(I32))

        nc.sync.dma_start(ka_l[:], ka)
        load_bytes(d_byte_tab, d_scales)
        nc.sync.dma_start(kb_l[:], kb)
        load_bytes(x_byte_tab, x_scales)
        nc.sync.dma_start(offs_l[:], offs)
        nc.sync.dma_start(gs_col[:], gs.rearrange("(p t) o -> p (t o)", t=4))
        load_words(x_word_tab, x_words)
        load_words(d_word_tab, d_words)
        nc.sync.dma_start(cand_l[:], cand)
        nc.sync.dma_start(n1_l[:], n1)
        nc.sync.dma_start(n2_l[:], n2)

        place = {
            "xq0_w": 1536, "xc0_w": 1280, "xc0_b": 1792,
            "zt0": 2048, "xq1_b": 2048,
            "grouped0": 4096, "xc2_w": 3136, "xc1_w": 4160, "xc1_b": 4672, "xc2_b": 4800, "xq1_w": 5056,
        }

        def tile(shape, dtype, name):
            if name in place:
                return share.tile(shape, dtype, name=name, align_bytes=64, offset=place[name])
            return keep.tile(shape, dtype, name=name, align_bytes=64)

        early_plane = tile([P, 2 * H + P], U8, "early_plane")
        nc.vector.memset(early_plane[:].bitcast(I32), 0)
        ident = keep.tile([P, P], F32, name="ident")
        make_identity(nc, ident[:])
        nc.gpsimd.memset(x_byte_rows[:].bitcast(I32), 0)
        for q in range(4):
            nc.gpsimd.dma_start(
                x_byte_rows[32 * q : 32 * q + 4, :].bitcast(I32), x_scales[0, 4 * q : 4 * q + 4, :].bitcast(I32)
            )

        gs_ps = psum.tile([P, 4, P], F32, name="gs_ps", tag="turn", bufs=2)
        for t in range(4):
            nc.tensor.transpose(gs_ps[:, t, :], gs_col[:, t : t + 1].to_broadcast([P, P]), ident[:])
        gs_row = keep.tile([P, 2, P, 2], F32, name="gs_row")
        nc.scalar.activation(gs_row[:], gs_ps[:].rearrange("p (u e) m -> p u m e", e=2), COPY, scale=SIXTEENTH)

        def gather(dst, tab, lst, start, n):
            nc.vector.tensor_copy(dst, tab[:].indirect(cols(lst, start, n)))

        def to_plane(plane, picked):
            for i in range(4):
                nc.sync.dma_start(plane[i:P:32, :].bitcast(I32), picked[8 * i : P : 32, :].bitcast(I32))

        early_bytes = tile([P, 2 * H + P], U8, "early_bytes")
        gather(early_bytes[:, 0:H], d_byte_tab, ka_l, 0, H)
        gather(early_bytes[:, H : 2 * H], d_byte_tab, kb_l, 0, H)
        gather(early_bytes[:, 2 * H : 2 * H + P], x_byte_tab, offs_l, 0, P)
        to_plane(early_plane, early_bytes)

        def pick_words(tab, lst, start, n, name):
            w = tile([P, n], U32, name)
            gather(w[:], tab, lst, start, n)
            return w

        def pick_x(lst, start, n, name):
            b = tile([P, n], U8, name + "_b")
            gather(b[:], x_byte_rows, lst, start, n)
            return pick_words(x_word_tab, lst, start, n, name + "_w"), b

        xq0_w = pick_words(x_word_tab, offs_l, 0, P, "xq0_w")
        d_a = pick_words(d_word_tab, ka_l, 0, H, "d_a")
        d_b = [pick_words(d_word_tab, kb_l, f * (H // 2), H // 2, "d_b%d" % f) for f in range(2)]

        def first_product(w, b, f, j, bank):
            n = H // 2
            words = (d_a[:, f * n : (f + 1) * n], d_b[f][:])[j]
            nc.tensor.matmul_mx(
                out=bank,
                lhsT=w.bitcast(FP8X4),
                lhsT_scale=b,
                rhs=words.bitcast(FP8X4),
                rhs_scale=early_plane[:, j * H + f * n : j * H + (f + 1) * n],
                start=(j == 0),
                stop=(j == 1),
            )

        def weigh(zt, bank, f0, n):
            m = slice(f0 // 4, (f0 + n) // 4)
            nc.vector.tensor_tensor(
                zt[:, :, m, :], bank.rearrange("p (m u e) -> p u m e", u=2, e=2), gs_row[:, :, m, :], MULT
            )

        def turn_and_quantize(zt, half):
            words = zt[:].rearrange("p u m e -> p (u m e)").bitcast(F32)
            turned = psum.tile([P, 2, P], F32, name="turned%d" % half, tag="turn", bufs=2)
            for u in range(2):
                nc.tensor.transpose(turned[:, u, :], words[:, u * P : (u + 1) * P], ident[:])
            grouped = tile([P, 4 * P], BF16, "grouped%d" % half)
            dst = grouped[:].bitcast(F32).rearrange("p (r u) -> p r u", u=2)
            src = turned[:].rearrange("p u r -> p r u")
            if half == 0:
                nc.scalar.copy(dst, src)
            else:
                nc.vector.tensor_copy(dst, src)
            zw = tile([P, P], U32, "zw%d" % half)
            zb = tile([P, P], U8, "zb%d" % half)
            nc.vector.quantize_mx(out=zw[:].bitcast(FP8X4), scales=zb[:], in_=grouped[:])
            return zw, zb

        sent = [
            [keep.tile([P, S], F32, name="sent%d_%d" % (c, j)) for j in range(2)] for c in range(C // P)
        ]

        def score_and_send(c, half, xc, z):
            bank = psum.tile([P, P], F32, name="s_ps", tag="s_ps", bufs=3)
            nc.tensor.matmul_mx(
                out=bank[:],
                lhsT=xc[0].bitcast(FP8X4),
                lhsT_scale=xc[1],
                rhs=z[0][:].bitcast(FP8X4),
                rhs_scale=z[1][:],
                start=True,
                stop=True,
            )
            s_sb = tile([P, P], F32, "s%d_%d" % (c, half))
            if c == 0 and half == 0:
                nc.scalar.activation(s_sb[:], bank[:], COPY, scale=SIXTEENTH)
            else:
                nc.vector.tensor_scalar(s_sb[:], bank[:], SIXTEENTH, None, MULT)
            for j, lst in enumerate((n1_l, n2_l)):
                nc.scalar.activation(sent[c][j][:].indirect(cols(lst, half * P, P)), s_sb[:], COPY)

        zt0 = tile([P, 2, P, 2], BF16, "zt0")
        banks = [psum.tile([P, H // 2], F32, name="h0_%d" % f) for f in range(2)]
        for j in range(2):
            for f in range(2):
                first_product(xq0_w[:], early_plane[:, 2 * H : 2 * H + P], f, j, banks[f][:])
        for f in range(2):
            weigh(zt0, banks[f][:], f * (H // 2), H // 2)
        w, b = pick_x(cand_l, 0, P, "xc0")
        xc = [(w[:], b[:])]
        z0 = turn_and_quantize(zt0, 0)
        score_and_send(0, 0, xc[0], z0)
        w, b = pick_x(cand_l, P, P, "xc1")
        xc.append((w[:], b[:]))
        score_and_send(1, 0, xc[1], z0)
        xq1_w, xq1_b = pick_x(offs_l, P, P, "xq1")
        w, b = pick_x(cand_l, 2 * P, 2 * P, "xc2")
        for c in range(2):
            xc.append((w[:, c * P : (c + 1) * P], b[:, c * P : (c + 1) * P]))
            score_and_send(2 + c, 0, xc[2 + c], z0)
        bank1 = psum.tile([P, H], F32, name="h1")
        for f in range(2):
            for j in range(2):
                first_product(xq1_w[:], xq1_b[:], f, j, bank1[:, f * (H // 2) : (f + 1) * (H // 2)])
        zt1 = tile([P, 2, P, 2], BF16, "zt1")
        weigh(zt1, bank1[:], 0, H)
        z1 = turn_and_quantize(zt1, 1)
        for c in range(C // P):
            score_and_send(c, 1, xc[c], z1)
            res = keep.tile([P, S], F32, name="res%d" % c)
            nc.vector.tensor_tensor(res[:], sent[c][0][:], sent[c][1][:], MAX)
            nc.sync.dma_start(out[c * P : (c + 1) * P, :], res[:])
